import numpy as np
import ml_dtypes


def mxq(x, axis, fmt="e4m3"):
    dtype, down = {"e4m3": (ml_dtypes.float8_e4m3fn, 7), "e5m2": (ml_dtypes.float8_e5m2, 14)}[fmt]
    v = np.moveaxis(np.asarray(x, np.float32).astype(ml_dtypes.bfloat16).astype(np.float64), axis, -1)
    blocks = v.reshape(v.shape[:-1] + (-1, 32))
    amax = np.abs(blocks).max(-1, keepdims=True)
    byte = np.maximum(np.where(amax > 0, np.frexp(amax)[1] - 1 + 127, 0) - down, 1)
    scale = np.exp2(byte - 127.0)
    codes = (blocks / scale).astype(np.float32).astype(dtype).astype(np.float64)
    return np.moveaxis((codes * scale).reshape(v.shape), -1, axis)


WIDE = False


def mx_kscale(k):
    if not WIDE:
        return np.ones(k)
    levels = np.array([10, -10, 5, -5, 0])
    if k % 512:
        return np.exp2(np.random.permutation(np.resize(levels, k // 32))).repeat(32)
    a = np.empty((k // 512, 16))
    for p in range(k // 512):
        a[p, :8] = np.random.permutation(np.resize(levels, 8))
        for g in range(8):
            far = levels[np.abs(levels - a[p, g]) >= 10]
            a[p, g + 8] = far[np.random.randint(len(far))]
    return np.exp2(a.ravel()).repeat(32)


def f64(x):
    return np.asarray(x).astype(np.float64)


def striped(idx):
    return np.tile(idx.reshape(-1, 16).T, (8, 1)).astype(np.uint16)


def unstriped(offs):
    return offs[:16].T.reshape(-1).astype(np.int64)


def striped8(idx):
    return np.concatenate([x.reshape(-1, 16).T for x in idx]).astype(np.uint16)


def runs(offs, k):
    lists = np.stack([offs[16 * r : 16 * r + 16].T.reshape(-1) for r in range(8)]).astype(np.int64)
    return lists[np.arange(k) % 512 // 64]


def pack_weight(w):
    k, n = w.shape
    w = f64(np.asarray(w, np.float32).astype(ml_dtypes.bfloat16)).reshape(k // 32, 32, n)
    amax = np.abs(w).max(1)
    byte = np.clip(np.where(amax > 0, np.frexp(amax)[1] - 1 + 127 - 7, 1), 1, 254)
    scaled = (w * np.exp2(127.0 - byte)[:, None, :]).reshape(k, n).astype(np.float32)
    words = np.ascontiguousarray(scaled.reshape(k // 512, 128, 4, n).transpose(0, 1, 3, 2)).astype(ml_dtypes.float8_e4m3fn).view(np.uint8)
    return words, np.ascontiguousarray(byte.astype(np.uint8).reshape(k // 512, 16, n))


def unpack_weight(words, scales):
    g, p, n, _ = words.shape
    vals = np.ascontiguousarray(words).view(ml_dtypes.float8_e4m3fn).astype(np.float64) * np.repeat(np.exp2(scales.astype(np.float64) - 127.0), 8, axis=1)[..., None]
    return vals.transpose(0, 1, 3, 2).reshape(g * 512, n)


def sigmoid(v):
    return 1.0 / (1.0 + np.exp(-np.maximum(v, -700.0)))


K, T, S, H, W = 512, 2048, 512, 512, 256


def setup_inputs():
    n = np.random.standard_normal
    s = mx_kscale(K)[:, None]
    u = mx_kscale(H)
    packed_xT = pack_weight(n((K, T)) * s)
    perm = np.stack([np.random.permutation(S) for _ in range(8)])
    return {
        "x_words": packed_xT[0],
        "x_scales": packed_xT[1],
        "w1": (n((K, H)) / np.sqrt(K) / s).astype(np.float32),
        "gn": (np.random.uniform(0.5, 1.5, (H, 1)) * u[:, None]).astype(np.float32),
        "w2": (n((H, H)) / np.sqrt(H) / u[:, None]).astype(np.float32),
        "offs": striped(np.random.permutation(T)[:S]),
        "n1": striped8(np.stack([np.random.permutation(S) for _ in range(8)])),
        "n2": striped8(np.stack([np.random.permutation(S) for _ in range(8)])),
        "n3": striped8(np.stack([np.random.permutation(S) for _ in range(8)])),
        "n4": striped8(perm[:, :W]),
        "n5": striped8(perm[:, W:]),
        "n6": striped8(np.stack([np.random.permutation(S)[:W] for _ in range(8)])),
        "n7": striped8(np.stack([np.random.permutation(S)[:W] for _ in range(8)])),
    }


def reference(x_words, x_scales, w1, gn, w2, offs, n1, n2, n3, n4, n5, n6, n7):
    xq = unpack_weight(x_words, x_scales)[:, unstriped(offs)]
    y = mxq(f64(w1), 0, "e4m3").T @ xq
    pb = y[np.arange(H)[:, None], runs(n5, H)]
    pa = y[np.arange(H)[:, None], runs(n4, H)]
    rb = pb - (0.5 * pa)
    ra = np.sqrt((pa) ** 2 + (pb) ** 2 + 0.25)
    ds = np.zeros((H, S))
    ds[np.arange(H)[:, None], runs(n4, H)] = ra
    dt = ds.copy()
    dt[np.arange(H)[:, None], runs(n5, H)] = rb
    z2 = f64(gn) * dt
    w2q = mxq(f64(w2), 0, "e4m3")
    b = w2q.T @ mxq(z2, 0, "e4m3")
    z = f64(gn) * ((y[np.arange(H)[:, None], runs(n1, H)]) * sigmoid(y) + (y[np.arange(H)[:, None], runs(n2, H)]) * (sigmoid(y[np.arange(H)[:, None], runs(n3, H)])))
    a = w2q.T @ mxq(z, 0, "e4m3")
    ra2 = b[np.arange(H)[:, None], runs(n7, H)] - (0.5 * (a[np.arange(H)[:, None], runs(n6, H)]))
    out = a.copy()
    out[np.arange(H)[:, None], runs(n6, H)] = ra2
    return out

@@ -1,0 +1,205 @@
+import concourse.mybir as mybir
+
+K, T, S, H, W = 512, 2048, 512, 512, 256
+FLOPS = 3 * 2 * K * H * S
+
+F32 = mybir.dt.float32
+BF16 = mybir.dt.bfloat16
+I32 = mybir.dt.int32
+U32 = mybir.dt.uint32
+U16 = mybir.dt.uint16
+U8 = mybir.dt.uint8
+FP8X4 = mybir.dt.float8_e4m3fn_x4
+MULT = mybir.AluOpType.mult
+ADD = mybir.AluOpType.add
+ACT = mybir.ActivationFunctionType
+
+P = 128
+PACK = 4
+HALF = S // 2
+LIST_COLS = HALF // 16
+W1_SPLIT = 88
+
+
+def tile_picked_tieputbwsumpolar_none_p_kernel(tc, x_words, x_scales, w1, gn, w2, offs, n1, n2, n3, n4, n5, n6, n7, out):
+    nc = tc.nc
+    with (
+        tc.tile_pool(name="lists", bufs=1) as lists,
+        tc.tile_pool(name="keep", bufs=1) as keep,
+        tc.psum_pool(name="psum", bufs=1) as psum,
+    ):
+        def load_list(name, src):
+            tile = lists.tile(list(src.shape), U16, name=name)
+            nc.sync.dma_start(tile[:], src)
+            return tile
+
+        def half_of(tile, h):
+            return tile[:, h * LIST_COLS : (h + 1) * LIST_COLS]
+
+        def deal(engine_copy, grouped, raw, m0, m1):
+            engine_copy(
+                grouped[:].rearrange("p t m j -> p m t j")[:, m0:m1],
+                raw[:].rearrange("p j (m t) -> p m t j", t=PACK)[:, m0:m1],
+            )
+
+        def quantize(name, grouped_ap, width):
+            codes = keep.tile([P, width], U32, name=name + "_codes", align_bytes=64)
+            scales = keep.tile([P, width], U8, name=name + "_scales", align_bytes=64)
+            nc.vector.quantize_mx(out=codes[:].bitcast(FP8X4), scales=scales[:], in_=grouped_ap)
+            return codes, scales
+
+        def product(acc, w, t, x):
+            cols = slice(t * P, (t + 1) * P)
+            nc.tensor.matmul_mx(
+                out=acc,
+                lhsT=w[0][:, cols].bitcast(FP8X4),
+                lhsT_scale=w[1][:, cols],
+                rhs=x[0][:].bitcast(FP8X4),
+                rhs_scale=x[1][:],
+                start=True,
+                stop=True,
+            )
+
+        def scale_into_pairs(pairs, t, plane):
+            nc.scalar.activation(pairs[:, t // 2, :, t % 2], plane, ACT.Copy, scale=gains[:, t : t + 1])
+
+        def weave(name, pairs, width):
+            grouped = keep.tile([P, width * PACK], BF16, name=name + "_grouped", align_bytes=64)
+            nc.scalar.copy(
+                grouped[:].bitcast(F32).rearrange("p (s u) -> p s u", u=2),
+                pairs[:].rearrange("p u s e -> p u (s e)").bitcast(F32).rearrange("p u s -> p s u"),
+            )
+            return grouped
+
+        scale_table = keep.tile([P, T], U8, name="scale_table", align_bytes=64)
+        nc.vector.memset(scale_table[:].bitcast(I32), 0)
+        offs_t = load_list("offs_t", offs)
+        w1_raw = keep.tile([P, PACK, H], F32, name="w1_raw")
+        nc.sync.dma_start(w1_raw[:], w1.rearrange("(p j) c -> p j c", j=PACK))
+        word_table = keep.tile([P, T], I32, name="word_table", align_bytes=64)
+        nc.sync.dma_start(word_table[:], x_words[0].rearrange("p n t -> p (n t)").bitcast(I32))
+        for q in range(4):
+            nc.scalar.dma_start(
+                scale_table[:].bitcast(I32)[32 * q : 32 * q + 4, :], x_scales[0].bitcast(I32)[4 * q : 4 * q + 4, :]
+            )
+        n4_t = load_list("n4_t", n4)
+        n5_t = load_list("n5_t", n5)
+        n3_t = load_list("n3_t", n3)
+        w2_raw = keep.tile([P, PACK, H], F32, name="w2_raw")
+        nc.sync.dma_start(w2_raw[:], w2.rearrange("(p j) c -> p j c", j=PACK))
+        n1_t = load_list("n1_t", n1)
+        n2_t = load_list("n2_t", n2)
+        gains = keep.tile([P, PACK], F32, name="gains")
+        nc.sync.dma_start(gains[:], gn.rearrange("(p t) o -> p (t o)", t=PACK))
+        n7_t = load_list("n7_t", n7)
+        n6_t = load_list("n6_t", n6)
+
+        warm = keep.tile([P, 2], F32, name="warm")
+        nc.gpsimd.memset(warm[:], 0.0)
+        nc.scalar.activation(warm[:, 1:2], warm[:, 0:1], ACT.Sigmoid)
+
+        dt = [keep.tile([P, S], F32, name="dt%d" % t) for t in range(PACK)]
+        for t in range(PACK):
+            nc.gpsimd.memset(dt[t][:], 0.0)
+
+        x_sc = keep.tile([P, S], U8, name="x_sc", align_bytes=64)
+        nc.vector.tensor_copy(x_sc[:], scale_table[:].indirect(offs_t[:]))
+        w1_grouped = keep.tile([P, PACK, P, PACK], BF16, name="w1_grouped", align_bytes=64)
+        deal(nc.vector.tensor_copy, w1_grouped, w1_raw, 0, W1_SPLIT)
+        deal(nc.scalar.copy, w1_grouped, w1_raw, W1_SPLIT, P)
+        w1q = quantize("w1", w1_grouped[:].rearrange("p t m j -> p (t m j)"), H)
+        x_codes = keep.tile([P, S], U32, name="x_codes", align_bytes=64)
+        nc.vector.tensor_copy(x_codes[:], word_table[:].bitcast(U32).indirect(offs_t[:]))
+
+        y = []
+        for t in range(PACK):
+            acc = psum.tile([P, S], F32, name="y_acc%d" % t, tag="bank%d" % t)
+            product(acc[:], w1q, t, (x_codes, x_sc))
+            y.append(keep.tile([P, S], F32, name="y%d" % t))
+            nc.scalar.copy(y[t][:], acc[:])
+
+        ha, pb, qa, qb = [], [], [], []
+        for t in range(PACK):
+            ha.append(keep.tile([P, W], F32, name="ha%d" % t, tag="left%d" % t))
+            pb.append(keep.tile([P, W], F32, name="pb%d" % t, tag="right%d" % t))
+            qa.append(keep.tile([P, W], F32, name="qa%d" % t))
+            qb.append(keep.tile([P, W], F32, name="qb%d" % t))
+            nc.vector.tensor_scalar(ha[t][:], y[t][:].indirect(n4_t[:]), -0.5, 0.0, MULT, ADD)
+            nc.vector.tensor_copy(pb[t][:], y[t][:].indirect(n5_t[:]))
+            nc.scalar.activation(qa[t][:], ha[t][:], ACT.Square, scale=2.0)
+            nc.scalar.activation(qb[t][:], pb[t][:], ACT.Square)
+        for t in range(PACK):
+            nc.vector.tensor_tensor(dt[t][:].indirect(n4_t[:]), qa[t][:], qb[t][:], ADD)
+
+        own = [keep.tile([P, S], F32, name="own%d" % t) for t in range(PACK)]
+        far = [keep.tile([P, S], F32, name="far%d" % t) for t in range(PACK)]
+        for h in range(2):
+            cols = slice(h * HALF, (h + 1) * HALF)
+            for t in range(PACK):
+                nc.scalar.activation(own[t][:, cols], y[t][:, cols], ACT.Sigmoid)
+                nc.scalar.activation(far[t][:, cols], y[t][:].indirect(half_of(n3_t, h)), ACT.Sigmoid)
+        for t in range(PACK):
+            nc.scalar.activation(dt[t][:], dt[t][:], ACT.Sqrt, bias=0.25)
+
+        w2_grouped = keep.tile([P, PACK, P, PACK], BF16, name="w2_grouped", align_bytes=64)
+        deal(nc.scalar.copy, w2_grouped, w2_raw, 0, P)
+        w2q = quantize("w2", w2_grouped[:].rearrange("p t m j -> p (t m j)"), H)
+
+        a = [keep.tile([P, S], F32, name="a%d" % t) for t in range(PACK)]
+
+        def gated_half(h, tags):
+            cols = slice(h * HALF, (h + 1) * HALF)
+            pairs = keep.tile([P, 2, HALF, 2], BF16, name="z_pairs%d" % h, align_bytes=64)
+            for t in range(PACK):
+                left = keep.tile([P, HALF], F32, name="left%d_%d" % (h, t), tag=tags[0] % t)
+                right = keep.tile([P, HALF], F32, name="right%d_%d" % (h, t), tag=tags[1] % t)
+                total = keep.tile([P, HALF], F32, name="total%d_%d" % (h, t))
+                nc.vector.tensor_tensor(left[:], y[t][:].indirect(half_of(n1_t, h)), own[t][:, cols], MULT)
+                nc.vector.tensor_tensor(right[:], y[t][:].indirect(half_of(n2_t, h)), far[t][:, cols], MULT)
+                nc.vector.tensor_tensor(total[:], left[:], right[:], ADD)
+                scale_into_pairs(pairs, t, total[:])
+            return weave("z%d" % h, pairs, HALF)
+
+        def product_a(h, grouped):
+            cols = slice(h * HALF, (h + 1) * HALF)
+            zq = quantize("z%d" % h, grouped[:], HALF)
+            for u in range(2):
+                acc = psum.tile([P, 2, HALF], F32, name="a_acc%d_%d" % (h, u), tag="bank%d" % (2 * h + u))
+                for e in range(2):
+                    product(acc[:, e, :], w2q, 2 * u + e, zq)
+                for e in range(2):
+                    nc.scalar.copy(a[2 * u + e][:, cols], acc[:, e, :])
+
+        z_first = gated_half(0, ("first_left%d", "first_right%d"))
+
+        z2_pairs = keep.tile([P, 2, S, 2], BF16, name="z2_pairs", align_bytes=64)
+        for t in range(PACK):
+            nc.vector.tensor_tensor(dt[t][:].indirect(n5_t[:]), pb[t][:], ha[t][:], ADD)
+            scale_into_pairs(z2_pairs, t, dt[t][:])
+        z2_grouped = weave("z2", z2_pairs, S)
+        product_a(0, z_first)
+        z2q = quantize("zz", z2_grouped[:], S)
+        b = []
+        for t in range(PACK):
+            acc = psum.tile([P, S], F32, name="b_acc%d" % t, tag="bank%d" % (PACK + t))
+            product(acc[:], w2q, t, z2q)
+            b.append(keep.tile([P, S], F32, name="b%d" % t))
+            nc.scalar.copy(b[t][:], acc[:])
+
+        z_second = gated_half(1, ("left%d", "right%d"))
+        product_a(1, z_second)
+
+        picked_b = keep.tile([P, PACK, W], F32, name="picked_b", tag="right%d" % (PACK - 1))
+        for t in range(PACK):
+            nc.vector.tensor_copy(picked_b[:, t, :], b[t][:].indirect(n7_t[:]))
+
+        out_rows = out.rearrange("(p t) n -> p t n", t=PACK)
+        half_a = [keep.tile([P, W], F32, name="half_a%d" % t) for t in range(PACK)]
+        for t in range(PACK):
+            nc.vector.tensor_scalar(half_a[t][:], a[t][:].indirect(n6_t[:]), -0.5, 0.0, MULT, ADD)
+            if t > 0:
+                nc.vector.tensor_tensor(a[t - 1][:].indirect(n6_t[:]), picked_b[:, t - 1, :], half_a[t - 1][:], ADD)
+                nc.sync.dma_start(out_rows[:, t - 1, :], a[t - 1][:])
+        last = PACK - 1
+        nc.vector.tensor_tensor(a[last][:].indirect(n6_t[:]), picked_b[:, last, :], half_a[last][:], ADD)
+        nc.sync.dma_start(out_rows[:, last, :], a[last][:])

@@ -1,4 +1,5 @@
 import concourse.mybir as mybir
+from concourse.masks import make_identity
 
 K, T, S, H, W = 512, 2048, 512, 512, 256
 FLOPS = 3 * 2 * K * H * S
@@ -48,49 +49,39 @@ def tile_picked_tieputbwsumpolar_none_p_kernel(tc, x_words, x_scales, w1, gn, w2
             nc.vector.quantize_mx(out=codes[:].bitcast(FP8X4), scales=scales[:], in_=grouped_ap)
             return codes, scales
 
-        def product(acc, w, t, x):
+        def product(acc, w, t, x, x_cols):
             cols = slice(t * P, (t + 1) * P)
             nc.tensor.matmul_mx(
                 out=acc,
                 lhsT=w[0][:, cols].bitcast(FP8X4),
                 lhsT_scale=w[1][:, cols],
-                rhs=x[0][:].bitcast(FP8X4),
-                rhs_scale=x[1][:],
+                rhs=x[0][:, x_cols].bitcast(FP8X4),
+                rhs_scale=x[1][:, x_cols],
                 start=True,
                 stop=True,
             )
 
-        def scale_into_pairs(pairs, t, plane):
-            nc.scalar.activation(pairs[:, t // 2, :, t % 2], plane, ACT.Copy, scale=gains[:, t : t + 1])
-
-        def weave(name, pairs, width):
-            grouped = keep.tile([P, width * PACK], BF16, name=name + "_grouped", align_bytes=64)
-            nc.scalar.copy(
-                grouped[:].bitcast(F32).rearrange("p (s u) -> p s u", u=2),
-                pairs[:].rearrange("p u s e -> p u (s e)").bitcast(F32).rearrange("p u s -> p s u"),
-            )
-            return grouped
-
-        scale_table = keep.tile([P, T], U8, name="scale_table", align_bytes=64)
-        nc.vector.memset(scale_table[:].bitcast(I32), 0)
         offs_t = load_list("offs_t", offs)
+        scale_rows = keep.tile([P, T // 4], I32, name="scale_rows", align_bytes=64)
+        for q in range(4):
+            nc.sync.dma_start(scale_rows[32 * q : 32 * q + 4, :], x_scales[0].bitcast(I32)[4 * q : 4 * q + 4, :])
         w1_raw = keep.tile([P, PACK, H], F32, name="w1_raw")
         nc.sync.dma_start(w1_raw[:], w1.rearrange("(p j) c -> p j c", j=PACK))
         word_table = keep.tile([P, T], I32, name="word_table", align_bytes=64)
         nc.sync.dma_start(word_table[:], x_words[0].rearrange("p n t -> p (n t)").bitcast(I32))
+        scale_table = keep.tile([P, T], U8, name="scale_table", align_bytes=64)
+        nc.vector.memset(scale_table[:].bitcast(I32), 0)
         for q in range(4):
-            nc.scalar.dma_start(
-                scale_table[:].bitcast(I32)[32 * q : 32 * q + 4, :], x_scales[0].bitcast(I32)[4 * q : 4 * q + 4, :]
-            )
+            nc.vector.tensor_copy(scale_table[:].bitcast(I32)[32 * q : 32 * q + 4, :], scale_rows[32 * q : 32 * q + 4, :])
         n4_t = load_list("n4_t", n4)
         n5_t = load_list("n5_t", n5)
-        n3_t = load_list("n3_t", n3)
-        w2_raw = keep.tile([P, PACK, H], F32, name="w2_raw")
-        nc.sync.dma_start(w2_raw[:], w2.rearrange("(p j) c -> p j c", j=PACK))
-        n1_t = load_list("n1_t", n1)
-        n2_t = load_list("n2_t", n2)
         gains = keep.tile([P, PACK], F32, name="gains")
         nc.sync.dma_start(gains[:], gn.rearrange("(p t) o -> p (t o)", t=PACK))
+        n3_t = load_list("n3_t", n3)
+        n1_t = load_list("n1_t", n1)
+        n2_t = load_list("n2_t", n2)
+        w2_raw = keep.tile([P, PACK, H], F32, name="w2_raw")
+        nc.sync.dma_start(w2_raw[:], w2.rearrange("(p j) c -> p j c", j=PACK))
         n7_t = load_list("n7_t", n7)
         n6_t = load_list("n6_t", n6)
 
@@ -98,9 +89,11 @@ def tile_picked_tieputbwsumpolar_none_p_kernel(tc, x_words, x_scales, w1, gn, w2
         nc.gpsimd.memset(warm[:], 0.0)
         nc.scalar.activation(warm[:, 1:2], warm[:, 0:1], ACT.Sigmoid)
 
-        dt = [keep.tile([P, S], F32, name="dt%d" % t) for t in range(PACK)]
+        ds = [keep.tile([P, S], F32, name="ds%d" % t) for t in range(PACK)]
         for t in range(PACK):
-            nc.gpsimd.memset(dt[t][:], 0.0)
+            nc.gpsimd.memset(ds[t][:], 0.0)
+        ident = keep.tile([P, P], F32, name="ident")
+        make_identity(nc, ident[:])
 
         x_sc = keep.tile([P, S], U8, name="x_sc", align_bytes=64)
         nc.vector.tensor_copy(x_sc[:], scale_table[:].indirect(offs_t[:]))
@@ -109,97 +102,139 @@ def tile_picked_tieputbwsumpolar_none_p_kernel(tc, x_words, x_scales, w1, gn, w2
         deal(nc.scalar.copy, w1_grouped, w1_raw, W1_SPLIT, P)
         w1q = quantize("w1", w1_grouped[:].rearrange("p t m j -> p (t m j)"), H)
         x_codes = keep.tile([P, S], U32, name="x_codes", align_bytes=64)
-        nc.vector.tensor_copy(x_codes[:], word_table[:].bitcast(U32).indirect(offs_t[:]))
-
-        y = []
-        for t in range(PACK):
-            acc = psum.tile([P, S], F32, name="y_acc%d" % t, tag="bank%d" % t)
-            product(acc[:], w1q, t, (x_codes, x_sc))
-            y.append(keep.tile([P, S], F32, name="y%d" % t))
-            nc.scalar.copy(y[t][:], acc[:])
-
-        ha, pb, qa, qb = [], [], [], []
-        for t in range(PACK):
-            ha.append(keep.tile([P, W], F32, name="ha%d" % t, tag="left%d" % t))
-            pb.append(keep.tile([P, W], F32, name="pb%d" % t, tag="right%d" % t))
-            qa.append(keep.tile([P, W], F32, name="qa%d" % t))
-            qb.append(keep.tile([P, W], F32, name="qb%d" % t))
-            nc.vector.tensor_scalar(ha[t][:], y[t][:].indirect(n4_t[:]), -0.5, 0.0, MULT, ADD)
-            nc.vector.tensor_copy(pb[t][:], y[t][:].indirect(n5_t[:]))
-            nc.scalar.activation(qa[t][:], ha[t][:], ACT.Square, scale=2.0)
-            nc.scalar.activation(qb[t][:], pb[t][:], ACT.Square)
-        for t in range(PACK):
-            nc.vector.tensor_tensor(dt[t][:].indirect(n4_t[:]), qa[t][:], qb[t][:], ADD)
-
-        own = [keep.tile([P, S], F32, name="own%d" % t) for t in range(PACK)]
-        far = [keep.tile([P, S], F32, name="far%d" % t) for t in range(PACK)]
+        halves = [slice(h * HALF, (h + 1) * HALF) for h in range(2)]
         for h in range(2):
-            cols = slice(h * HALF, (h + 1) * HALF)
-            for t in range(PACK):
-                nc.scalar.activation(own[t][:, cols], y[t][:, cols], ACT.Sigmoid)
-                nc.scalar.activation(far[t][:, cols], y[t][:].indirect(half_of(n3_t, h)), ACT.Sigmoid)
-        for t in range(PACK):
-            nc.scalar.activation(dt[t][:], dt[t][:], ACT.Sqrt, bias=0.25)
+            nc.vector.tensor_copy(x_codes[:, halves[h]], word_table[:].bitcast(U32).indirect(half_of(offs_t, h)))
 
-        w2_grouped = keep.tile([P, PACK, P, PACK], BF16, name="w2_grouped", align_bytes=64)
+        y, y_acc = [], []
+        for t in range(PACK):
+            y_acc.append(psum.tile([P, S], F32, name="y_acc%d" % t, tag="bank%d" % t))
+            for h in range(2):
+                product(y_acc[t][:, halves[h]], w1q, t, (x_codes, x_sc), halves[h])
+            y.append(keep.tile([P, S], F32, name="y%d" % t, tag="y%d" % t))
+            nc.scalar.copy(y[t][:], y_acc[t][:])
+
+
+        wide = [keep.tile([P, 2 * S], F32, name="wide%d" % t) for t in range(PACK)]
+        ha = [wide[t][:, S : S + W] for t in range(PACK)]
+        pb = [wide[t][:, S + W : 2 * S] for t in range(PACK)]
+        for t in range(PACK):
+            nc.vector.tensor_scalar(ha[t], y[t][:].indirect(n4_t[:]), -0.5, 0.0, MULT, ADD)
+            nc.vector.tensor_copy(pb[t], y[t][:].indirect(n5_t[:]))
+
+        sums = [
+            [psum.tile([P, 2, 2, P], F32, name="sums%d_%d" % (u, h), tag="bank%d" % (4 + 2 * u + h)) for h in range(2)]
+            for u in range(2)
+        ]
+        for t in range(PACK):
+            own = keep.tile([P, S], F32, name="own%d" % t, tag="own%d" % t, align_bytes=64)
+            far = keep.tile([P, S], F32, name="far%d" % t)
+            left = keep.tile([P, S], F32, name="left%d" % t)
+            right = keep.tile([P, S], F32, name="right%d" % t)
+            nc.scalar.activation(wide[t][:, 0:S], y_acc[t][:], ACT.Copy, scale=gains[:, t : t + 1])
+            nc.scalar.activation(own[:], y[t][:], ACT.Sigmoid)
+            for h in range(2):
+                nc.scalar.activation(far[:, halves[h]], y[t][:].indirect(half_of(n3_t, h)), ACT.Sigmoid)
+            nc.vector.tensor_tensor(left[:], wide[t][:].indirect(n1_t[:]), own[:], MULT)
+            nc.vector.tensor_tensor(right[:], wide[t][:].indirect(n2_t[:]), far[:], MULT)
+            for c in range(PACK):
+                cols = slice(c * P, (c + 1) * P)
+                acc = sums[t // 2][c // 2][:, c % 2, t % 2, :]
+                nc.tensor.matmul(acc, left[:, cols], ident[:], start=True, stop=False, is_transpose=True)
+                nc.tensor.matmul(acc, right[:, cols], ident[:], start=False, stop=True, is_transpose=True)
+
+        for t in range(PACK):
+            squares = keep.tile([P, 2, W], F32, name="squares%d" % t, tag="y%d" % t)
+            nc.scalar.activation(squares[:, 0, :], ha[t], ACT.Square, scale=2.0)
+            nc.scalar.activation(squares[:, 1, :], pb[t], ACT.Square)
+            nc.vector.tensor_tensor(ds[t][:].indirect(n4_t[:]), squares[:, 0, :], squares[:, 1, :], ADD)
+
+        rows = [
+            [
+                keep.tile([P, 2, P, 2], BF16, name="rows%d_%d" % (u, h), tag="rows%d_%d" % (u, h), align_bytes=64)
+                for h in range(2)
+            ]
+            for u in range(2)
+        ]
+
+        def round_rows(u):
+            for h in range(2):
+                nc.scalar.copy(rows[u][h][:], sums[u][h][:].rearrange("s c e p -> s c p e"))
+
+        dt = []
+
+        def polar_plane(t, tag):
+            dt.append(keep.tile([P, S], F32, name="dt%d" % t, tag=tag, align_bytes=64))
+            nc.scalar.activation(dt[t][:], ds[t][:], ACT.Sqrt, bias=0.25)
+            nc.vector.tensor_tensor(dt[t][:].indirect(n5_t[:]), pb[t], ha[t], ADD)
+
+        round_rows(0)
+        w2_grouped = keep.tile([P, PACK, P, PACK], BF16, name="w2_grouped", tag="own3", align_bytes=64)
         deal(nc.scalar.copy, w2_grouped, w2_raw, 0, P)
         w2q = quantize("w2", w2_grouped[:].rearrange("p t m j -> p (t m j)"), H)
+        polar_plane(0, "dt0")
+        round_rows(1)
 
         a = [keep.tile([P, S], F32, name="a%d" % t) for t in range(PACK)]
-
-        def gated_half(h, tags):
-            cols = slice(h * HALF, (h + 1) * HALF)
-            pairs = keep.tile([P, 2, HALF, 2], BF16, name="z_pairs%d" % h, align_bytes=64)
-            for t in range(PACK):
-                left = keep.tile([P, HALF], F32, name="left%d_%d" % (h, t), tag=tags[0] % t)
-                right = keep.tile([P, HALF], F32, name="right%d_%d" % (h, t), tag=tags[1] % t)
-                total = keep.tile([P, HALF], F32, name="total%d_%d" % (h, t))
-                nc.vector.tensor_tensor(left[:], y[t][:].indirect(half_of(n1_t, h)), own[t][:, cols], MULT)
-                nc.vector.tensor_tensor(right[:], y[t][:].indirect(half_of(n2_t, h)), far[t][:, cols], MULT)
-                nc.vector.tensor_tensor(total[:], left[:], right[:], ADD)
-                scale_into_pairs(pairs, t, total[:])
-            return weave("z%d" % h, pairs, HALF)
-
-        def product_a(h, grouped):
-            cols = slice(h * HALF, (h + 1) * HALF)
-            zq = quantize("z%d" % h, grouped[:], HALF)
+        first_cols = slice(0, HALF)
+        for h in range(2):
+            back = psum.tile([P, 2, HALF], F32, name="back%d" % h, tag="bank%d" % h)
             for u in range(2):
-                acc = psum.tile([P, 2, HALF], F32, name="a_acc%d_%d" % (h, u), tag="bank%d" % (2 * h + u))
+                words = rows[u][h][:].rearrange("s c p e -> s c (p e)").bitcast(F32)
+                for c in range(2):
+                    nc.tensor.transpose(back[:, u, c * P : (c + 1) * P], words[:, c, :], ident[:])
+            grouped = keep.tile([P, HALF * PACK], BF16, name="z_grouped%d" % h, tag="z_grouped%d" % h, align_bytes=64)
+            nc.scalar.copy(grouped[:].bitcast(F32).rearrange("p (s u) -> p s u", u=2), back[:].rearrange("p u s -> p s u"))
+            zq = quantize("z%d" % h, grouped[:], HALF)
+            polar_plane(1 + h, "rows1_%d" % h)
+            if h == 1:
+                polar_plane(3, "z_grouped0")
+            for u in range(2):
+                acc = psum.tile([P, 2, HALF], F32, name="a_acc%d_%d" % (h, u), tag="bank%d" % (2 + 2 * h + u))
                 for e in range(2):
-                    product(acc[:, e, :], w2q, 2 * u + e, zq)
+                    product(acc[:, e, :], w2q, 2 * u + e, zq, first_cols)
                 for e in range(2):
-                    nc.scalar.copy(a[2 * u + e][:, cols], acc[:, e, :])
+                    nc.scalar.copy(a[2 * u + e][:, halves[h]], acc[:, e, :])
 
-        z_first = gated_half(0, ("first_left%d", "first_right%d"))
+        z2_pairs = keep.tile([P, 2, S, 2], BF16, name="z2_pairs", tag="z_grouped1", align_bytes=64)
 
-        z2_pairs = keep.tile([P, 2, S, 2], BF16, name="z2_pairs", align_bytes=64)
-        for t in range(PACK):
-            nc.vector.tensor_tensor(dt[t][:].indirect(n5_t[:]), pb[t][:], ha[t][:], ADD)
-            scale_into_pairs(z2_pairs, t, dt[t][:])
-        z2_grouped = weave("z2", z2_pairs, S)
-        product_a(0, z_first)
-        z2q = quantize("zz", z2_grouped[:], S)
-        b = []
-        for t in range(PACK):
-            acc = psum.tile([P, S], F32, name="b_acc%d" % t, tag="bank%d" % (PACK + t))
-            product(acc[:], w2q, t, z2q)
-            b.append(keep.tile([P, S], F32, name="b%d" % t))
-            nc.scalar.copy(b[t][:], acc[:])
+        def scale_into_pairs(t, cols):
+            nc.scalar.activation(z2_pairs[:, t // 2, cols, t % 2], dt[t][:, cols], ACT.Copy, scale=gains[:, t : t + 1])
 
-        z_second = gated_half(1, ("left%d", "right%d"))
-        product_a(1, z_second)
+        for t in range(PACK - 1):
+            scale_into_pairs(t, slice(0, S))
 
-        picked_b = keep.tile([P, PACK, W], F32, name="picked_b", tag="right%d" % (PACK - 1))
-        for t in range(PACK):
-            nc.vector.tensor_copy(picked_b[:, t, :], b[t][:].indirect(n7_t[:]))
+        z2_words = z2_pairs[:].rearrange("p u s e -> p u (s e)").bitcast(F32).rearrange("p u s -> p s u")
+        b_acc = []
+        for h in range(2):
+            scale_into_pairs(3, halves[h])
+            grouped = keep.tile([P, HALF * PACK], BF16, name="z2_grouped%d" % h, tag="z2_grouped%d" % h, align_bytes=64)
+            nc.scalar.copy(grouped[:].bitcast(F32).rearrange("p (s u) -> p s u", u=2), z2_words[:, halves[h], :])
+            z2q = quantize("zz%d" % h, grouped[:], HALF)
+            for u in range(2):
+                acc = psum.tile([P, 2, HALF], F32, name="b_acc%d_%d" % (h, u), tag="bank%d" % ((6 + 2 * h + u) % 8))
+                for e in range(2):
+                    product(acc[:, e, :], w2q, 2 * u + e, z2q, slice(0, HALF))
+                b_acc.append(acc)
+
+        half_a = []
+        for t, tag in enumerate(("half_a0", "half_a1", "z2_grouped0", "z2_grouped1")):
+            half_a.append(keep.tile([P, W], F32, name="half_a%d" % t, tag=tag, align_bytes=64))
+            nc.vector.tensor_scalar(half_a[t][:], a[t][:].indirect(n6_t[:]), -0.5, 0.0, MULT, ADD)
 
         out_rows = out.rearrange("(p t) n -> p t n", t=PACK)
-        half_a = [keep.tile([P, W], F32, name="half_a%d" % t) for t in range(PACK)]
+        picked_b = []
+
+        def finish(t):
+            nc.vector.tensor_tensor(a[t][:].indirect(n6_t[:]), picked_b[t][:], half_a[t][:], ADD)
+            nc.sync.dma_start(out_rows[:, t, :], a[t][:])
+
         for t in range(PACK):
-            nc.vector.tensor_scalar(half_a[t][:], a[t][:].indirect(n6_t[:]), -0.5, 0.0, MULT, ADD)
+            b = keep.tile([P, S], F32, name="b%d" % t)
+            for h in range(2):
+                nc.scalar.copy(b[:, halves[h]], b_acc[2 * h + t // 2][:, t % 2, :])
+            picked_b.append(keep.tile([P, W], F32, name="picked_b%d" % t))
+            nc.vector.tensor_copy(picked_b[t][:], b[:].indirect(n7_t[:]))
             if t > 0:
-                nc.vector.tensor_tensor(a[t - 1][:].indirect(n6_t[:]), picked_b[:, t - 1, :], half_a[t - 1][:], ADD)
-                nc.sync.dma_start(out_rows[:, t - 1, :], a[t - 1][:])
-        last = PACK - 1
-        nc.vector.tensor_tensor(a[last][:].indirect(n6_t[:]), picked_b[:, last, :], half_a[last][:], ADD)
-        nc.sync.dma_start(out_rows[:, last, :], a[last][:])
+                finish(t - 1)
+        finish(PACK - 1)

@@ -91,7 +91,7 @@ def tile_picked_tieputbwsumpolar_none_p_kernel(tc, x_words, x_scales, w1, gn, w2
 
         ds = [keep.tile([P, S], F32, name="ds%d" % t) for t in range(PACK)]
         for t in range(PACK):
-            nc.gpsimd.memset(ds[t][:], 0.0)
+            nc.vector.memset(ds[t][:], 0.0)
         ident = keep.tile([P, P], F32, name="ident")
         make_identity(nc, ident[:])
 
@@ -114,8 +114,11 @@ def tile_picked_tieputbwsumpolar_none_p_kernel(tc, x_words, x_scales, w1, gn, w2
             y.append(keep.tile([P, S], F32, name="y%d" % t, tag="y%d" % t))
             nc.scalar.copy(y[t][:], y_acc[t][:])
 
+        w2_grouped = keep.tile([P, PACK, P, PACK], BF16, name="w2_grouped", align_bytes=64)
+        deal(lambda dst, src: nc.gpsimd.tensor_scalar(dst, src, 1.0, 0.0, MULT, ADD), w2_grouped, w2_raw, 0, P)
+        w2q = quantize("w2", w2_grouped[:].rearrange("p t m j -> p (t m j)"), H)
 
-        wide = [keep.tile([P, 2 * S], F32, name="wide%d" % t) for t in range(PACK)]
+        wide = [keep.tile([P, 2 * S], F32, name="wide%d" % t, tag="wide%d" % t) for t in range(PACK)]
         ha = [wide[t][:, S : S + W] for t in range(PACK)]
         pb = [wide[t][:, S + W : 2 * S] for t in range(PACK)]
         for t in range(PACK):
@@ -127,7 +130,7 @@ def tile_picked_tieputbwsumpolar_none_p_kernel(tc, x_words, x_scales, w1, gn, w2
             for u in range(2)
         ]
         for t in range(PACK):
-            own = keep.tile([P, S], F32, name="own%d" % t, tag="own%d" % t, align_bytes=64)
+            own = keep.tile([P, S], F32, name="own%d" % t)
             far = keep.tile([P, S], F32, name="far%d" % t)
             left = keep.tile([P, S], F32, name="left%d" % t)
             right = keep.tile([P, S], F32, name="right%d" % t)
@@ -169,15 +172,12 @@ def tile_picked_tieputbwsumpolar_none_p_kernel(tc, x_words, x_scales, w1, gn, w2
             nc.vector.tensor_tensor(dt[t][:].indirect(n5_t[:]), pb[t], ha[t], ADD)
 
         round_rows(0)
-        w2_grouped = keep.tile([P, PACK, P, PACK], BF16, name="w2_grouped", tag="own3", align_bytes=64)
-        deal(nc.scalar.copy, w2_grouped, w2_raw, 0, P)
-        w2q = quantize("w2", w2_grouped[:].rearrange("p t m j -> p (t m j)"), H)
-        polar_plane(0, "dt0")
         round_rows(1)
 
         a = [keep.tile([P, S], F32, name="a%d" % t) for t in range(PACK)]
-        first_cols = slice(0, HALF)
-        for h in range(2):
+        zq = []
+
+        def quantize_z(h):
             back = psum.tile([P, 2, HALF], F32, name="back%d" % h, tag="bank%d" % h)
             for u in range(2):
                 words = rows[u][h][:].rearrange("s c p e -> s c (p e)").bitcast(F32)
@@ -185,54 +185,72 @@ def tile_picked_tieputbwsumpolar_none_p_kernel(tc, x_words, x_scales, w1, gn, w2
                     nc.tensor.transpose(back[:, u, c * P : (c + 1) * P], words[:, c, :], ident[:])
             grouped = keep.tile([P, HALF * PACK], BF16, name="z_grouped%d" % h, tag="z_grouped%d" % h, align_bytes=64)
             nc.scalar.copy(grouped[:].bitcast(F32).rearrange("p (s u) -> p s u", u=2), back[:].rearrange("p u s -> p s u"))
-            zq = quantize("z%d" % h, grouped[:], HALF)
-            polar_plane(1 + h, "rows1_%d" % h)
-            if h == 1:
-                polar_plane(3, "z_grouped0")
+            zq.append(quantize("z%d" % h, grouped[:], HALF))
+
+        def product_a(h):
             for u in range(2):
                 acc = psum.tile([P, 2, HALF], F32, name="a_acc%d_%d" % (h, u), tag="bank%d" % (2 + 2 * h + u))
                 for e in range(2):
-                    product(acc[:, e, :], w2q, 2 * u + e, zq, first_cols)
+                    product(acc[:, e, :], w2q, 2 * u + e, zq[h], slice(0, HALF))
                 for e in range(2):
                     nc.scalar.copy(a[2 * u + e][:, halves[h]], acc[:, e, :])
 
-        z2_pairs = keep.tile([P, 2, S, 2], BF16, name="z2_pairs", tag="z_grouped1", align_bytes=64)
+        z2_pairs = keep.tile([P, 2, S, 2], BF16, name="z2_pairs", align_bytes=64)
 
         def scale_into_pairs(t, cols):
             nc.scalar.activation(z2_pairs[:, t // 2, cols, t % 2], dt[t][:, cols], ACT.Copy, scale=gains[:, t : t + 1])
 
-        for t in range(PACK - 1):
-            scale_into_pairs(t, slice(0, S))
+        quantize_z(0)
+        polar_plane(0, "rows1_0")
+        quantize_z(1)
+        polar_plane(1, "rows1_1")
+        polar_plane(2, "z_grouped0")
+        product_a(0)
+        polar_plane(3, "z_grouped1")
+        scale_into_pairs(0, slice(0, S))
+        product_a(1)
+        scale_into_pairs(1, slice(0, S))
+        scale_into_pairs(2, slice(0, S))
 
         z2_words = z2_pairs[:].rearrange("p u s e -> p u (s e)").bitcast(F32).rearrange("p u s -> p s u")
-        b_acc = []
+        z2_grouped = keep.tile([P, S * PACK], BF16, name="z2_grouped", tag="z2_grouped", align_bytes=64)
+        z2_woven = z2_grouped[:].bitcast(F32).rearrange("p (s u) -> p s u", u=2)
+        z2q = (
+            keep.tile([P, S], U32, name="z2_codes", align_bytes=64),
+            keep.tile([P, S], U8, name="z2_scales", align_bytes=64),
+        )
         for h in range(2):
-            scale_into_pairs(3, halves[h])
-            grouped = keep.tile([P, HALF * PACK], BF16, name="z2_grouped%d" % h, tag="z2_grouped%d" % h, align_bytes=64)
-            nc.scalar.copy(grouped[:].bitcast(F32).rearrange("p (s u) -> p s u", u=2), z2_words[:, halves[h], :])
-            z2q = quantize("zz%d" % h, grouped[:], HALF)
-            for u in range(2):
-                acc = psum.tile([P, 2, HALF], F32, name="b_acc%d_%d" % (h, u), tag="bank%d" % ((6 + 2 * h + u) % 8))
-                for e in range(2):
-                    product(acc[:, e, :], w2q, 2 * u + e, z2q, slice(0, HALF))
-                b_acc.append(acc)
-
-        half_a = []
-        for t, tag in enumerate(("half_a0", "half_a1", "z2_grouped0", "z2_grouped1")):
-            half_a.append(keep.tile([P, W], F32, name="half_a%d" % t, tag=tag, align_bytes=64))
-            nc.vector.tensor_scalar(half_a[t][:], a[t][:].indirect(n6_t[:]), -0.5, 0.0, MULT, ADD)
+            scale_into_pairs(PACK - 1, halves[h])
+        half_a_early = keep.tile([P, 2, W], F32, name="half_a_early", tag="wide3")
+        for e in range(2):
+            nc.vector.tensor_scalar(half_a_early[:, e, :], a[e][:].indirect(n6_t[:]), -0.5, 0.0, MULT, ADD)
+        nc.scalar.copy(z2_woven[:, halves[0], :], z2_words[:, halves[0], :])
+        nc.vector.tensor_copy(z2_woven[:, halves[1], :], z2_words[:, halves[1], :])
+        for h in range(2):
+            nc.vector.quantize_mx(
+                out=z2q[0][:, halves[h]].bitcast(FP8X4),
+                scales=z2q[1][:, halves[h]],
+                in_=z2_grouped[:, h * HALF * PACK : (h + 1) * HALF * PACK],
+            )
+        half_a_late = keep.tile([P, 2, W], F32, name="half_a_late", tag="z2_grouped", align_bytes=64)
+        for e in range(2):
+            nc.vector.tensor_scalar(half_a_late[:, e, :], a[2 + e][:].indirect(n6_t[:]), -0.5, 0.0, MULT, ADD)
+        half_a = [half_a_early[:, 0, :], half_a_early[:, 1, :], half_a_late[:, 0, :], half_a_late[:, 1, :]]
 
         out_rows = out.rearrange("(p t) n -> p t n", t=PACK)
         picked_b = []
 
         def finish(t):
-            nc.vector.tensor_tensor(a[t][:].indirect(n6_t[:]), picked_b[t][:], half_a[t][:], ADD)
+            nc.vector.tensor_tensor(a[t][:].indirect(n6_t[:]), picked_b[t][:], half_a[t], ADD)
             nc.sync.dma_start(out_rows[:, t, :], a[t][:])
 
         for t in range(PACK):
             b = keep.tile([P, S], F32, name="b%d" % t)
-            for h in range(2):
-                nc.scalar.copy(b[:, halves[h]], b_acc[2 * h + t // 2][:, t % 2, :])
+            pieces = [("bank7", halves[1]), ("bank6", halves[0])] if t == 0 else [("bank%d" % (t - 1), slice(0, S))]
+            for tag, cols in pieces:
+                acc = psum.tile([P, S], F32, name="b_acc%d" % t, tag=tag)
+                product(acc[:, cols], w2q, t, z2q, cols)
+                nc.scalar.copy(b[:, cols], acc[:, cols])
             picked_b.append(keep.tile([P, W], F32, name="picked_b%d" % t))
             nc.vector.tensor_copy(picked_b[t][:], b[:].indirect(n7_t[:]))
             if t > 0:

import concourse.mybir as mybir
from concourse.masks import make_identity

K, T, S, H, W = 512, 2048, 512, 512, 256
FLOPS = 3 * 2 * K * H * S

F32 = mybir.dt.float32
BF16 = mybir.dt.bfloat16
I32 = mybir.dt.int32
U32 = mybir.dt.uint32
U16 = mybir.dt.uint16
U8 = mybir.dt.uint8
FP8X4 = mybir.dt.float8_e4m3fn_x4
MULT = mybir.AluOpType.mult
ADD = mybir.AluOpType.add
ACT = mybir.ActivationFunctionType

P = 128
PACK = 4
HALF = S // 2
LIST_COLS = HALF // 16
W1_SPLIT = 88


def tile_picked_tieputbwsumpolar_none_p_kernel(tc, x_words, x_scales, w1, gn, w2, offs, n1, n2, n3, n4, n5, n6, n7, out):
    nc = tc.nc
    with (
        tc.tile_pool(name="lists", bufs=1) as lists,
        tc.tile_pool(name="keep", bufs=1) as keep,
        tc.psum_pool(name="psum", bufs=1) as psum,
    ):
        def load_list(name, src):
            tile = lists.tile(list(src.shape), U16, name=name)
            nc.sync.dma_start(tile[:], src)
            return tile

        def half_of(tile, h):
            return tile[:, h * LIST_COLS : (h + 1) * LIST_COLS]

        def deal(engine_copy, grouped, raw, m0, m1):
            engine_copy(
                grouped[:].rearrange("p t m j -> p m t j")[:, m0:m1],
                raw[:].rearrange("p j (m t) -> p m t j", t=PACK)[:, m0:m1],
            )

        def quantize(name, grouped_ap, width):
            codes = keep.tile([P, width], U32, name=name + "_codes", align_bytes=64)
            scales = keep.tile([P, width], U8, name=name + "_scales", align_bytes=64)
            nc.vector.quantize_mx(out=codes[:].bitcast(FP8X4), scales=scales[:], in_=grouped_ap)
            return codes, scales

        def product(acc, w, t, x, x_cols):
            cols = slice(t * P, (t + 1) * P)
            nc.tensor.matmul_mx(
                out=acc,
                lhsT=w[0][:, cols].bitcast(FP8X4),
                lhsT_scale=w[1][:, cols],
                rhs=x[0][:, x_cols].bitcast(FP8X4),
                rhs_scale=x[1][:, x_cols],
                start=True,
                stop=True,
            )

        offs_t = load_list("offs_t", offs)
        scale_rows = keep.tile([P, T // 4], I32, name="scale_rows", align_bytes=64)
        for q in range(4):
            nc.sync.dma_start(scale_rows[32 * q : 32 * q + 4, :], x_scales[0].bitcast(I32)[4 * q : 4 * q + 4, :])
        w1_raw = keep.tile([P, PACK, H], F32, name="w1_raw")
        nc.sync.dma_start(w1_raw[:], w1.rearrange("(p j) c -> p j c", j=PACK))
        word_table = keep.tile([P, T], I32, name="word_table", align_bytes=64)
        nc.sync.dma_start(word_table[:], x_words[0].rearrange("p n t -> p (n t)").bitcast(I32))
        scale_table = keep.tile([P, T], U8, name="scale_table", align_bytes=64)
        nc.vector.memset(scale_table[:].bitcast(I32), 0)
        for q in range(4):
            nc.vector.tensor_copy(scale_table[:].bitcast(I32)[32 * q : 32 * q + 4, :], scale_rows[32 * q : 32 * q + 4, :])
        n4_t = load_list("n4_t", n4)
        n5_t = load_list("n5_t", n5)
        gains = keep.tile([P, PACK], F32, name="gains")
        nc.sync.dma_start(gains[:], gn.rearrange("(p t) o -> p (t o)", t=PACK))
        n3_t = load_list("n3_t", n3)
        n1_t = load_list("n1_t", n1)
        n2_t = load_list("n2_t", n2)
        w2_raw = keep.tile([P, PACK, H], F32, name="w2_raw")
        nc.sync.dma_start(w2_raw[:], w2.rearrange("(p j) c -> p j c", j=PACK))
        n7_t = load_list("n7_t", n7)
        n6_t = load_list("n6_t", n6)

        warm = keep.tile([P, 2], F32, name="warm")
        nc.gpsimd.memset(warm[:], 0.0)
        nc.scalar.activation(warm[:, 1:2], warm[:, 0:1], ACT.Sigmoid)

        ds = [keep.tile([P, S], F32, name="ds%d" % t) for t in range(PACK)]
        for t in range(PACK):
            nc.vector.memset(ds[t][:], 0.0)
        ident = keep.tile([P, P], F32, name="ident")
        make_identity(nc, ident[:])

        x_sc = keep.tile([P, S], U8, name="x_sc", align_bytes=64)
        nc.vector.tensor_copy(x_sc[:], scale_table[:].indirect(offs_t[:]))
        w1_grouped = keep.tile([P, PACK, P, PACK], BF16, name="w1_grouped", align_bytes=64)
        deal(nc.vector.tensor_copy, w1_grouped, w1_raw, 0, W1_SPLIT)
        deal(nc.scalar.copy, w1_grouped, w1_raw, W1_SPLIT, P)
        w1q = quantize("w1", w1_grouped[:].rearrange("p t m j -> p (t m j)"), H)
        x_codes = keep.tile([P, S], U32, name="x_codes", align_bytes=64)
        halves = [slice(h * HALF, (h + 1) * HALF) for h in range(2)]
        for h in range(2):
            nc.vector.tensor_copy(x_codes[:, halves[h]], word_table[:].bitcast(U32).indirect(half_of(offs_t, h)))

        y, y_acc = [], []
        for t in range(PACK):
            y_acc.append(psum.tile([P, S], F32, name="y_acc%d" % t, tag="bank%d" % t))
            for h in range(2):
                product(y_acc[t][:, halves[h]], w1q, t, (x_codes, x_sc), halves[h])
            y.append(keep.tile([P, S], F32, name="y%d" % t, tag="y%d" % t))
            nc.scalar.copy(y[t][:], y_acc[t][:])

        w2_grouped = keep.tile([P, PACK, P, PACK], BF16, name="w2_grouped", align_bytes=64)
        deal(lambda dst, src: nc.gpsimd.tensor_scalar(dst, src, 1.0, 0.0, MULT, ADD), w2_grouped, w2_raw, 0, P)
        w2q = quantize("w2", w2_grouped[:].rearrange("p t m j -> p (t m j)"), H)

        wide = [keep.tile([P, 2 * S], F32, name="wide%d" % t, tag="wide%d" % t) for t in range(PACK)]
        ha = [wide[t][:, S : S + W] for t in range(PACK)]
        pb = [wide[t][:, S + W : 2 * S] for t in range(PACK)]
        for t in range(PACK):
            nc.vector.tensor_scalar(ha[t], y[t][:].indirect(n4_t[:]), -0.5, 0.0, MULT, ADD)
            nc.vector.tensor_copy(pb[t], y[t][:].indirect(n5_t[:]))

        sums = [
            [psum.tile([P, 2, 2, P], F32, name="sums%d_%d" % (u, h), tag="bank%d" % (4 + 2 * u + h)) for h in range(2)]
            for u in range(2)
        ]
        for t in range(PACK):
            own = keep.tile([P, S], F32, name="own%d" % t)
            far = keep.tile([P, S], F32, name="far%d" % t)
            left = keep.tile([P, S], F32, name="left%d" % t)
            right = keep.tile([P, S], F32, name="right%d" % t)
            nc.scalar.activation(wide[t][:, 0:S], y_acc[t][:], ACT.Copy, scale=gains[:, t : t + 1])
            nc.scalar.activation(own[:], y[t][:], ACT.Sigmoid)
            for h in range(2):
                nc.scalar.activation(far[:, halves[h]], y[t][:].indirect(half_of(n3_t, h)), ACT.Sigmoid)
            nc.vector.tensor_tensor(left[:], wide[t][:].indirect(n1_t[:]), own[:], MULT)
            nc.vector.tensor_tensor(right[:], wide[t][:].indirect(n2_t[:]), far[:], MULT)
            for c in range(PACK):
                cols = slice(c * P, (c + 1) * P)
                acc = sums[t // 2][c // 2][:, c % 2, t % 2, :]
                nc.tensor.matmul(acc, left[:, cols], ident[:], start=True, stop=False, is_transpose=True)
                nc.tensor.matmul(acc, right[:, cols], ident[:], start=False, stop=True, is_transpose=True)

        for t in range(PACK):
            squares = keep.tile([P, 2, W], F32, name="squares%d" % t, tag="y%d" % t)
            nc.scalar.activation(squares[:, 0, :], ha[t], ACT.Square, scale=2.0)
            nc.scalar.activation(squares[:, 1, :], pb[t], ACT.Square)
            nc.vector.tensor_tensor(ds[t][:].indirect(n4_t[:]), squares[:, 0, :], squares[:, 1, :], ADD)

        rows = [
            [
                keep.tile([P, 2, P, 2], BF16, name="rows%d_%d" % (u, h), tag="rows%d_%d" % (u, h), align_bytes=64)
                for h in range(2)
            ]
            for u in range(2)
        ]

        def round_rows(u):
            for h in range(2):
                nc.scalar.copy(rows[u][h][:], sums[u][h][:].rearrange("s c e p -> s c p e"))

        dt = []

        def polar_plane(t, tag):
            dt.append(keep.tile([P, S], F32, name="dt%d" % t, tag=tag, align_bytes=64))
            nc.scalar.activation(dt[t][:], ds[t][:], ACT.Sqrt, bias=0.25)
            nc.vector.tensor_tensor(dt[t][:].indirect(n5_t[:]), pb[t], ha[t], ADD)

        round_rows(0)
        round_rows(1)

        a = [keep.tile([P, S], F32, name="a%d" % t) for t in range(PACK)]
        zq = []

        def quantize_z(h):
            back = psum.tile([P, 2, HALF], F32, name="back%d" % h, tag="bank%d" % h)
            for u in range(2):
                words = rows[u][h][:].rearrange("s c p e -> s c (p e)").bitcast(F32)
                for c in range(2):
                    nc.tensor.transpose(back[:, u, c * P : (c + 1) * P], words[:, c, :], ident[:])
            grouped = keep.tile([P, HALF * PACK], BF16, name="z_grouped%d" % h, tag="z_grouped%d" % h, align_bytes=64)
            nc.scalar.copy(grouped[:].bitcast(F32).rearrange("p (s u) -> p s u", u=2), back[:].rearrange("p u s -> p s u"))
            zq.append(quantize("z%d" % h, grouped[:], HALF))

        def product_a(h):
            for u in range(2):
                acc = psum.tile([P, 2, HALF], F32, name="a_acc%d_%d" % (h, u), tag="bank%d" % (2 + 2 * h + u))
                for e in range(2):
                    product(acc[:, e, :], w2q, 2 * u + e, zq[h], slice(0, HALF))
                for e in range(2):
                    nc.scalar.copy(a[2 * u + e][:, halves[h]], acc[:, e, :])

        z2_pairs = keep.tile([P, 2, S, 2], BF16, name="z2_pairs", align_bytes=64)

        def scale_into_pairs(t, cols):
            nc.scalar.activation(z2_pairs[:, t // 2, cols, t % 2], dt[t][:, cols], ACT.Copy, scale=gains[:, t : t + 1])

        quantize_z(0)
        polar_plane(0, "rows1_0")
        quantize_z(1)
        polar_plane(1, "rows1_1")
        polar_plane(2, "z_grouped0")
        product_a(0)
        polar_plane(3, "z_grouped1")
        scale_into_pairs(0, slice(0, S))
        product_a(1)
        scale_into_pairs(1, slice(0, S))
        scale_into_pairs(2, slice(0, S))

        z2_words = z2_pairs[:].rearrange("p u s e -> p u (s e)").bitcast(F32).rearrange("p u s -> p s u")
        z2_grouped = keep.tile([P, S * PACK], BF16, name="z2_grouped", tag="z2_grouped", align_bytes=64)
        z2_woven = z2_grouped[:].bitcast(F32).rearrange("p (s u) -> p s u", u=2)
        z2q = (
            keep.tile([P, S], U32, name="z2_codes", align_bytes=64),
            keep.tile([P, S], U8, name="z2_scales", align_bytes=64),
        )
        for h in range(2):
            scale_into_pairs(PACK - 1, halves[h])
        half_a_early = keep.tile([P, 2, W], F32, name="half_a_early", tag="wide3")
        for e in range(2):
            nc.vector.tensor_scalar(half_a_early[:, e, :], a[e][:].indirect(n6_t[:]), -0.5, 0.0, MULT, ADD)
        nc.scalar.copy(z2_woven[:, halves[0], :], z2_words[:, halves[0], :])
        nc.vector.tensor_copy(z2_woven[:, halves[1], :], z2_words[:, halves[1], :])
        for h in range(2):
            nc.vector.quantize_mx(
                out=z2q[0][:, halves[h]].bitcast(FP8X4),
                scales=z2q[1][:, halves[h]],
                in_=z2_grouped[:, h * HALF * PACK : (h + 1) * HALF * PACK],
            )
        half_a_late = keep.tile([P, 2, W], F32, name="half_a_late", tag="z2_grouped", align_bytes=64)
        for e in range(2):
            nc.vector.tensor_scalar(half_a_late[:, e, :], a[2 + e][:].indirect(n6_t[:]), -0.5, 0.0, MULT, ADD)
        half_a = [half_a_early[:, 0, :], half_a_early[:, 1, :], half_a_late[:, 0, :], half_a_late[:, 1, :]]

        out_rows = out.rearrange("(p t) n -> p t n", t=PACK)
        picked_b = []

        def finish(t):
            nc.vector.tensor_tensor(a[t][:].indirect(n6_t[:]), picked_b[t][:], half_a[t], ADD)
            nc.sync.dma_start(out_rows[:, t, :], a[t][:])

        for t in range(PACK):
            b = keep.tile([P, S], F32, name="b%d" % t)
            pieces = [("bank7", halves[1]), ("bank6", halves[0])] if t == 0 else [("bank%d" % (t - 1), slice(0, S))]
            for tag, cols in pieces:
                acc = psum.tile([P, S], F32, name="b_acc%d" % t, tag=tag)
                product(acc[:, cols], w2q, t, z2q, cols)
                nc.scalar.copy(b[:, cols], acc[:, cols])
            picked_b.append(keep.tile([P, W], F32, name="picked_b%d" % t))
            nc.vector.tensor_copy(picked_b[t][:], b[:].indirect(n7_t[:]))
            if t > 0:
                finish(t - 1)
        finish(PACK - 1)
